import numpy as np
import ml_dtypes


def mxq(x, axis, fmt="e4m3"):
    dtype, down = {"e4m3": (ml_dtypes.float8_e4m3fn, 7), "e5m2": (ml_dtypes.float8_e5m2, 14)}[fmt]
    v = np.moveaxis(np.asarray(x, np.float32).astype(ml_dtypes.bfloat16).astype(np.float64), axis, -1)
    blocks = v.reshape(v.shape[:-1] + (-1, 32))
    amax = np.abs(blocks).max(-1, keepdims=True)
    byte = np.maximum(np.where(amax > 0, np.frexp(amax)[1] - 1 + 127, 0) - down, 1)
    scale = np.exp2(byte - 127.0)
    codes = (blocks / scale).astype(np.float32).astype(dtype).astype(np.float64)
    return np.moveaxis((codes * scale).reshape(v.shape), -1, axis)


WIDE = False


def mx_kscale(k):
    if not WIDE:
        return np.ones(k)
    levels = np.array([10, -10, 5, -5, 0])
    if k % 512:
        return np.exp2(np.random.permutation(np.resize(levels, k // 32))).repeat(32)
    a = np.empty((k // 512, 16))
    for p in range(k // 512):
        a[p, :8] = np.random.permutation(np.resize(levels, 8))
        for g in range(8):
            far = levels[np.abs(levels - a[p, g]) >= 10]
            a[p, g + 8] = far[np.random.randint(len(far))]
    return np.exp2(a.ravel()).repeat(32)


def f64(x):
    return np.asarray(x).astype(np.float64)


def striped(idx):
    return np.tile(np.asarray(idx).reshape(-1, 16).T, (8, 1)).astype(np.uint16)


def unstriped(offs):
    return offs[:16].T.reshape(-1).astype(np.int64)


E2M1 = np.array([0.0, 0.5, 1.0, 1.5, 2.0, 3.0, 4.0, 6.0, -0.0, -0.5, -1.0, -1.5, -2.0, -3.0, -4.0, -6.0])


def pack_weight(w, fmt):
    k, n = w.shape
    w = f64(np.asarray(w, np.float32).astype(ml_dtypes.bfloat16)).reshape(k // 32, 32, n)
    amax = np.abs(w).max(1)
    if fmt == "e4m3":
        byte = np.frexp(amax)[1] - 1 + 127 - 7
    else:
        mant, ex = np.frexp(amax / 6.0)
        byte = np.where(mant > 0.5, ex, ex - 1) + 127
    byte = np.clip(np.where(amax > 0, byte, 1), 1, 254)
    scaled = (w * np.exp2(127.0 - byte)[:, None, :]).reshape(k, n).astype(np.float32)
    by_word = np.ascontiguousarray(scaled.reshape(k // 512, 128, 4, n).transpose(0, 1, 3, 2))
    if fmt == "e4m3":
        words = by_word.astype(ml_dtypes.float8_e4m3fn).view(np.uint8)
    else:
        c = by_word.astype(ml_dtypes.float4_e2m1fn).view(np.uint8) & 0xF
        words = (c[..., 0::2] | (c[..., 1::2] << 4)).reshape(k // 512, 128, 2 * n)
    return np.ascontiguousarray(words), np.ascontiguousarray(byte.astype(np.uint8).reshape(k // 512, 16, n))


def unpack_weight(words, scales, fmt):
    g, _, n = scales.shape
    words = np.ascontiguousarray(words).reshape(g, 128, n, -1)
    if fmt == "e4m3":
        vals = words.view(ml_dtypes.float8_e4m3fn).astype(np.float64)
    else:
        nib = np.empty((g, 128, n, 4), np.uint8)
        nib[..., 0::2] = words & 0xF
        nib[..., 1::2] = words >> 4
        vals = E2M1[nib]
    vals = vals * np.repeat(np.exp2(scales.astype(np.float64) - 127.0), 8, axis=1)[..., None]
    return vals.transpose(0, 1, 3, 2).reshape(g * 512, n)


def sigmoid(v):
    return 1.0 / (1.0 + np.exp(-v))


D, E, T, I, Q, G = 512, 512, 2048, 512, 128, 32


def setup_inputs():
    n = np.random.standard_normal
    idx = np.random.permutation(T)[:I]
    fd = mx_kscale(D)
    fe = mx_kscale(E)
    keysp = pack_weight(n((D, T)) / fd[:, None], "e4m3")
    valsp = pack_weight(n((E, T)) / fe[:, None], "e4m3")
    return {
        "query": (n((D, Q)) * 0.8 / np.sqrt(D) * fd[:, None]).astype(np.float32),
        "keys_words": keysp[0],
        "keys_scales": keysp[1],
        "th": (np.random.uniform(-0.5, 0.5, (Q, 1))).astype(np.float32),
        "sharp": (np.random.uniform(1.0, 3.0, (Q, 1))).astype(np.float32),
        "gout": (n((E, Q)) * 1 / np.sqrt(E) * fe[:, None]).astype(np.float32),
        "vals_words": valsp[0],
        "vals_scales": valsp[1],
        "dquery": (n((D, Q)) * 1.0 / np.sqrt(D) * fd[:, None]).astype(np.float32),
        "base": (0.5 * n((Q, T))).astype(np.float32),
        "offs": striped(idx),
    }


def reference(query, keys_words, keys_scales, th, sharp, gout, vals_words, vals_scales, dquery, base, offs):
    idx = unstriped(offs)
    keysu = unpack_weight(keys_words, keys_scales, "e4m3")
    valsu = unpack_weight(vals_words, vals_scales, "e4m3")
    queryq = mxq(f64(query), 0, "e4m3")
    keysidxg = keysu[:, idx]
    a = queryq.T @ keysidxg
    dqueryq = mxq(f64(dquery), 0, "e4m3")
    ta = dqueryq.T @ keysidxg
    s = a.reshape(Q, G, I // G).mean(axis=2) * f64(sharp)
    p = np.exp(s - np.max(s, axis=1, keepdims=True))
    z = np.sum(p, axis=1, keepdims=True)
    r = p / z
    rr = np.repeat(r, I // G, axis=1)
    goutq = mxq(f64(gout), 0, "e4m3")
    valsidxg = valsu[:, idx]
    c0 = goutq.T @ valsidxg
    drr = c0 * sigmoid(a - f64(th))
    dr = drr.reshape(Q, G, I // G).sum(axis=2)
    dz = np.sum(dr * p / np.square(z) * (-1.0), axis=1, keepdims=True)
    dp = dr / z + dz
    ts = ta.reshape(Q, G, I // G).mean(axis=2) * f64(sharp)
    tp = ts * p
    tz = np.sum(tp, axis=1, keepdims=True)
    tr = (tp - tz * p / z) / z
    trr = np.repeat(tr, I // G, axis=1)
    tdrr = ta * sigmoid(a - f64(th)) * (1.0 - sigmoid(a - f64(th))) * c0
    tdr = tdrr.reshape(Q, G, I // G).sum(axis=2)
    tdz = np.sum((tdr * p + tp * dr - tz * z * 2.0 * dr * p / np.square(z)) / np.square(z) * (-1.0), axis=1, keepdims=True)
    tdp = (tdr - tz * dr / z) / z + tdz
    tds = tdp * p + tp * dp
    te1 = tds * f64(sharp) / 16.0
    tr1 = np.repeat(te1, I // G, axis=1)
    tda = (trr * c0 * sigmoid(a - f64(th)) + ta * sigmoid(a - f64(th)) * (1.0 - sigmoid(a - f64(th))) * c0 * rr) * (1.0 - sigmoid(a - f64(th))) + ta * sigmoid(a - f64(th)) * (1.0 - sigmoid(a - f64(th))) * (-1.0) * c0 * rr * sigmoid(a - f64(th)) + tr1
    gs = tda * 32.0
    gf = np.zeros((Q, T))
    gf[:, idx] = gs
    y = f64(base) + gf
    return y

@@ -1,0 +1,215 @@
+from contextlib import ExitStack
+
+import concourse.mybir as mybir
+
+F32 = mybir.dt.float32
+BF16 = mybir.dt.bfloat16
+I32 = mybir.dt.int32
+U32 = mybir.dt.uint32
+U16 = mybir.dt.uint16
+U8 = mybir.dt.uint8
+FP8X4 = mybir.dt.float8_e4m3fn_x4
+ALU = mybir.AluOpType
+ACT = mybir.ActivationFunctionType
+AX = mybir.AxisListType
+
+P = 128
+PACK = 4
+TOKENS = 2048
+SLOTS = 512
+PAGE = 16
+PAGES = SLOTS // PAGE
+HALVES = 2
+HS = SLOTS // HALVES
+HP = PAGES // HALVES
+VAL_ROW = 4
+OUT_CHUNKS = [256, 512, 512, 512, 256]
+
+FLOPS = 3 * 2 * 512 * 128 * 512
+
+
+def tile_attend_hvpagetimessigmoid_s_kernel(tc, query, keys_words, keys_scales, th, sharp, gout, vals_words, vals_scales, dquery, base, offs, out):
+    nc = tc.nc
+    with ExitStack() as ctx:
+        held = ctx.enter_context(tc.tile_pool(name="held", bufs=1))
+        psum = ctx.enter_context(tc.psum_pool(name="psum", bufs=1))
+
+        def small(name, width=1):
+            return held.tile([P, width], F32, name=name)
+
+        def wide(name):
+            return held.tile([P, SLOTS], F32, name=name)
+
+        def by_page(ap):
+            return ap.rearrange("p (g j) -> p g j", j=PAGE)
+
+        def spread(ap):
+            return ap.unsqueeze(2).to_broadcast([P, ap.shape[1], PAGE])
+
+        offsets = held.tile([P, SLOTS // 16], U16, name="offsets")
+        key_words = held.tile([P, TOKENS], U32, name="key_words", tag="pool_then_base")
+        key_bytes = held.tile([P, TOKENS], U8, name="key_bytes", tag="bytes_then_vals")
+        window = held.tile([P, TOKENS], F32, name="window")
+        th_col = small("th_col")
+        sharp_col = small("sharp_col")
+
+        nc.vector.memset(key_bytes[:].bitcast(I32), 0)
+
+        warm = small("warm")
+        warm_out = small("warm_out")
+        nc.vector.memset(warm[:], 0.0)
+        nc.vector.memset(window[:], 0.0)
+
+        for quad in range(4):
+            nc.scalar.dma_start(out=key_bytes[32 * quad : 32 * quad + 4, :].bitcast(I32), in_=keys_scales[0, 4 * quad : 4 * quad + 4, :].bitcast(I32))
+        nc.scalar.activation(warm_out[:], warm[:], ACT.Exp)
+        nc.sync.dma_start(offsets[:], offs)
+        nc.gpsimd.dma_start(out=th_col[:], in_=th)
+        nc.gpsimd.dma_start(out=sharp_col[:], in_=sharp)
+
+        def load_rows(rows, name, tag):
+            staged = held.tile([P, PACK, P], F32, name=name, tag=tag, align_bytes=64)
+            nc.sync.dma_start(out=staged[:], in_=rows.rearrange("(p t) q -> p t q", t=PACK))
+            return staged
+
+        def quantise(staged, name):
+            woven = held.tile([P, P, PACK], BF16, name=name + "_woven", tag=name + "_woven", align_bytes=64)
+            codes = held.tile([P, P], U32, name=name + "_codes", tag=name + "_codes", align_bytes=64)
+            scales = held.tile([P, P], U8, name=name + "_scales", align_bytes=64)
+            nc.scalar.copy(out=woven[:], in_=staged[:].rearrange("p t q -> p q t"))
+            nc.vector.quantize_mx(out=codes[:].bitcast(FP8X4), scales=scales[:], in_=woven[:].rearrange("p q t -> p (q t)"))
+            return codes, scales
+
+        q_staged = load_rows(query, "q_staged", "q_staged")
+        nc.sync.dma_start(out=key_words[:].bitcast(I32), in_=keys_words[0].rearrange("p n t -> p (n t)").bitcast(I32))
+        dq_staged = load_rows(dquery, "dq_staged", "dq_staged")
+
+        key_scale = held.tile([P, SLOTS], U8, name="key_scale", align_bytes=64)
+        nc.vector.tensor_copy(key_scale[:], key_bytes[:].indirect(offsets[:]))
+        q_codes, q_scales = quantise(q_staged, "q")
+        g_staged = load_rows(gout, "g_staged", "q_woven")
+        val_words = held.tile([P, TOKENS], U32, name="val_words", tag="bytes_then_vals")
+        nc.sync.dma_start(out=val_words[:].bitcast(I32), in_=vals_words[0].rearrange("p n t -> p (n t)").bitcast(I32))
+        val_bytes = held.tile([P, TOKENS], U8, name="val_bytes", tag="q_staged", align_bytes=64)
+        nc.vector.memset(val_bytes[:].bitcast(I32), 0)
+        for quad in range(4):
+            nc.scalar.dma_start(out=val_bytes[32 * quad + VAL_ROW : 32 * quad + VAL_ROW + 4, :].bitcast(I32), in_=vals_scales[0, 4 * quad : 4 * quad + 4, :].bitcast(I32))
+        dq_codes, dq_scales = quantise(dq_staged, "dq")
+
+        def gather_words(pool_words, h, name):
+            picked = held.tile([P, HS], U32, name=name + str(h), align_bytes=64)
+            nc.vector.tensor_copy(picked[:], pool_words[:].indirect(offsets[:, h * (HS // 16) : (h + 1) * (HS // 16)]))
+            return picked
+
+        def product(codes, scales, picked, picked_scale, name):
+            acc = psum.tile([P, HS], F32, name=name)
+            nc.tensor.matmul_mx(out=acc[:], lhsT=codes[:].bitcast(FP8X4), lhsT_scale=scales[:], rhs=picked[:].bitcast(FP8X4), rhs_scale=picked_scale, start=True, stop=True)
+            return acc
+
+        slots = [slice(h * HS, (h + 1) * HS) for h in range(HALVES)]
+        pages = [slice(h * HP, (h + 1) * HP) for h in range(HALVES)]
+
+        keys = [gather_words(key_words, h, "keys") for h in range(HALVES)]
+        a = [product(q_codes, q_scales, keys[h], key_scale[:, slots[h]], "a" + str(h)) for h in range(HALVES)]
+        ta = [product(dq_codes, dq_scales, keys[h], key_scale[:, slots[h]], "ta" + str(h)) for h in range(HALVES)]
+
+        base_sum = held.tile([P, TOKENS], F32, name="base_sum", tag="pool_then_base")
+        nc.sync.dma_start(out=base_sum[:], in_=base)
+
+        nth = small("nth")
+        sh16 = small("sh16")
+        nsh16 = small("nsh16")
+        nc.gpsimd.tensor_scalar(nth[:], th_col[:], -0.5, 0.0, ALU.mult, ALU.add)
+        nc.gpsimd.tensor_scalar(nsh16[:], sharp_col[:], -1.0 / PAGE, 0.0, ALU.mult, ALU.add)
+        nc.gpsimd.tensor_scalar(sh16[:], sharp_col[:], 1.0 / PAGE, 0.0, ALU.mult, ALU.add)
+
+
+        t = wide("t")
+        tt = wide("tt")
+        a_sum = small("a_sum", PAGES)
+        ta_sum = small("ta_sum", PAGES)
+        for h in range(HALVES):
+            nc.vector.tensor_reduce(a_sum[:, pages[h]], by_page(a[h][:]), AX.X, ALU.add)
+        for h in range(HALVES):
+            nc.scalar.activation(t[:, slots[h]], a[h][:], ACT.Tanh, bias=nth[:], scale=0.5)
+        neg_s = small("neg_s", PAGES)
+        neg_max = small("neg_max")
+        nc.vector.tensor_scalar(neg_s[:], a_sum[:], nsh16[:], None, ALU.mult, ALU.min, accum_out=neg_max[:])
+        p = small("p", PAGES)
+        z = small("z")
+        nc.scalar.activation(p[:], neg_s[:], ACT.Exp, bias=neg_max[:], scale=-1.0, accum_out=z[:])
+        nc.scalar.activation(tt[:], t[:], ACT.Square)
+        for h in range(HALVES):
+            nc.vector.tensor_reduce(ta_sum[:, pages[h]], by_page(ta[h][:]), AX.X, ALU.add)
+        g_codes, g_scales = quantise(g_staged, "g")
+
+        inv_z = small("inv_z")
+        tp = small("tp", PAGES)
+        tz = small("tz")
+        r = small("r", PAGES)
+        ts_mean = small("ts_mean")
+        v = small("v", PAGES)
+        v2s = small("v2s", PAGES)
+        nc.vector.reciprocal(inv_z[:], z[:])
+        nc.vector.scalar_tensor_tensor(tp[:], ta_sum[:], sh16[:], p[:], ALU.mult, ALU.mult, accum_out=tz[:])
+        ta_t = wide("ta_t")
+        for h in range(HALVES):
+            nc.vector.tensor_tensor(ta_t[:, slots[h]], ta[h][:], t[:, slots[h]], ALU.mult)
+        nc.vector.tensor_scalar(r[:], p[:], inv_z[:], None, ALU.mult)
+        nc.vector.tensor_scalar(ts_mean[:], tz[:], inv_z[:], None, ALU.mult)
+        nc.vector.tensor_scalar(v[:], ta_sum[:], sh16[:], ts_mean[:], ALU.mult, ALU.subtract)
+        nc.vector.tensor_scalar(v2s[:], v[:], sh16[:], 2.0, ALU.mult, ALU.mult)
+        r8 = wide("r8")
+        nc.scalar.activation(by_page(r8[:]), spread(r[:]), ACT.Copy, scale=8.0)
+
+        val_scale = held.tile([P, SLOTS], U8, name="val_scale", tag="dq_codes", align_bytes=64)
+        nc.vector.tensor_copy(val_scale[:], val_bytes[:].indirect(offsets[:]))
+        vals = [gather_words(val_words, h, "vals") for h in range(HALVES)]
+        c = [product(g_codes, g_scales, vals[h], val_scale[VAL_ROW:P, slots[h]], "c" + str(h)) for h in range(HALVES)]
+
+        shifted = wide("shifted")
+        nc.vector.tensor_tensor(by_page(shifted[:]), by_page(ta_t[:]), spread(v[:]), ALU.subtract)
+
+        gated = wide("gated")
+        curved = wide("curved")
+        moved = wide("moved")
+        dr2 = small("dr2", PAGES)
+        tdr4 = small("tdr4", PAGES)
+        for h in range(HALVES):
+            nc.vector.scalar_tensor_tensor(curved[:, slots[h]], tt[:, slots[h]], 1.0, c[h][:], ALU.subtract, ALU.mult)
+        for h in range(HALVES):
+            nc.vector.scalar_tensor_tensor(gated[:, slots[h]], t[:, slots[h]], 1.0, c[h][:], ALU.add, ALU.mult)
+        for h in range(HALVES):
+            nc.vector.tensor_tensor(moved[:, slots[h]], ta[h][:], curved[:, slots[h]], ALU.mult)
+        nc.vector.tensor_reduce(dr2[:], by_page(gated[:]), AX.X, ALU.add)
+        nc.vector.tensor_reduce(tdr4[:], by_page(moved[:]), AX.X, ALU.add)
+
+        r_dr = small("r_dr", PAGES)
+        dr_mean = small("dr_mean")
+        e = small("e", PAGES)
+        r_e = small("r_e", PAGES)
+        e_mean = small("e_mean")
+        e_centred = small("e_centred", PAGES)
+        x = small("x", PAGES)
+        r_tdr = small("r_tdr", PAGES)
+        tdr_mean = small("tdr_mean")
+        local = wide("local")
+        nc.vector.scalar_tensor_tensor(r_dr[:], dr2[:], 1.0, r[:], ALU.mult, ALU.mult, accum_out=dr_mean[:])
+        nc.vector.scalar_tensor_tensor(e[:], dr2[:], dr_mean[:], v2s[:], ALU.subtract, ALU.mult)
+        nc.vector.scalar_tensor_tensor(r_e[:], e[:], 1.0, r[:], ALU.mult, ALU.mult, accum_out=e_mean[:])
+        nc.vector.tensor_scalar(e_centred[:], e[:], e_mean[:], None, ALU.subtract)
+        nc.vector.scalar_tensor_tensor(r_tdr[:], tdr4[:], nsh16[:], r[:], ALU.mult, ALU.mult, accum_out=tdr_mean[:])
+        nc.vector.scalar_tensor_tensor(x[:], tdr4[:], nsh16[:], e_centred[:], ALU.mult, ALU.add)
+        nc.vector.tensor_tensor(local[:], shifted[:], curved[:], ALU.mult)
+
+        total = wide("total")
+        nc.vector.scalar_tensor_tensor(by_page(total[:]), spread(x[:]), tdr_mean[:], by_page(local[:]), ALU.subtract, ALU.add)
+        nc.vector.tensor_tensor(window[:].indirect(offsets[:]), total[:], r8[:], ALU.mult)
+
+        start = 0
+        for n, width in enumerate(OUT_CHUNKS):
+            cols = slice(start, start + width)
+            nc.vector.tensor_tensor(base_sum[:, cols], base_sum[:, cols], window[:, cols], ALU.add)
+            queue = nc.sync if n % 2 == 0 else nc.scalar
+            queue.dma_start(out=out[:, cols], in_=base_sum[:, cols])
+            start = start + width

@@ -19,9 +19,6 @@ TOKENS = 2048
 SLOTS = 512
 PAGE = 16
 PAGES = SLOTS // PAGE
-HALVES = 2
-HS = SLOTS // HALVES
-HP = PAGES // HALVES
 VAL_ROW = 4
 OUT_CHUNKS = [256, 512, 512, 512, 256]
 
@@ -32,10 +29,11 @@ def tile_attend_hvpagetimessigmoid_s_kernel(tc, query, keys_words, keys_scales, 
     nc = tc.nc
     with ExitStack() as ctx:
         held = ctx.enter_context(tc.tile_pool(name="held", bufs=1))
+        early = ctx.enter_context(tc.tile_pool(name="early", bufs=1))
         psum = ctx.enter_context(tc.psum_pool(name="psum", bufs=1))
 
-        def small(name, width=1):
-            return held.tile([P, width], F32, name=name)
+        def small(name, width=1, tag=None):
+            return held.tile([P, width], F32, name=name, tag=tag or name, align_bytes=64)
 
         def wide(name):
             return held.tile([P, SLOTS], F32, name=name)
@@ -44,166 +42,155 @@ def tile_attend_hvpagetimessigmoid_s_kernel(tc, query, keys_words, keys_scales, 
             return ap.rearrange("p (g j) -> p g j", j=PAGE)
 
         def spread(ap):
-            return ap.unsqueeze(2).to_broadcast([P, ap.shape[1], PAGE])
+            return ap.unsqueeze(2).to_broadcast([P, PAGES, PAGE])
 
-        offsets = held.tile([P, SLOTS // 16], U16, name="offsets")
-        key_words = held.tile([P, TOKENS], U32, name="key_words", tag="pool_then_base")
-        key_bytes = held.tile([P, TOKENS], U8, name="key_bytes", tag="bytes_then_vals")
-        window = held.tile([P, TOKENS], F32, name="window")
-        th_col = small("th_col")
-        sharp_col = small("sharp_col")
+        def load_words(pool_words, words):
+            nc.sync.dma_start(out=pool_words[:].bitcast(I32), in_=words[0].rearrange("p n t -> p (n t)").bitcast(I32))
 
-        nc.vector.memset(key_bytes[:].bitcast(I32), 0)
+        def load_bytes(queue, pool_bytes, scale_rows, first):
+            for quad in range(4):
+                queue.dma_start(out=pool_bytes[32 * quad + first : 32 * quad + first + 4, :].bitcast(I32), in_=scale_rows[0, 4 * quad : 4 * quad + 4, :].bitcast(I32))
 
-        warm = small("warm")
-        warm_out = small("warm_out")
-        nc.vector.memset(warm[:], 0.0)
-        nc.vector.memset(window[:], 0.0)
-
-        for quad in range(4):
-            nc.scalar.dma_start(out=key_bytes[32 * quad : 32 * quad + 4, :].bitcast(I32), in_=keys_scales[0, 4 * quad : 4 * quad + 4, :].bitcast(I32))
-        nc.scalar.activation(warm_out[:], warm[:], ACT.Exp)
-        nc.sync.dma_start(offsets[:], offs)
-        nc.gpsimd.dma_start(out=th_col[:], in_=th)
-        nc.gpsimd.dma_start(out=sharp_col[:], in_=sharp)
-
-        def load_rows(rows, name, tag):
-            staged = held.tile([P, PACK, P], F32, name=name, tag=tag, align_bytes=64)
+        def load_rows(staged, rows):
             nc.sync.dma_start(out=staged[:], in_=rows.rearrange("(p t) q -> p t q", t=PACK))
-            return staged
 
-        def quantise(staged, name):
-            woven = held.tile([P, P, PACK], BF16, name=name + "_woven", tag=name + "_woven", align_bytes=64)
+        def quantise(staged, woven, name):
             codes = held.tile([P, P], U32, name=name + "_codes", tag=name + "_codes", align_bytes=64)
             scales = held.tile([P, P], U8, name=name + "_scales", align_bytes=64)
             nc.scalar.copy(out=woven[:], in_=staged[:].rearrange("p t q -> p q t"))
             nc.vector.quantize_mx(out=codes[:].bitcast(FP8X4), scales=scales[:], in_=woven[:].rearrange("p q t -> p (q t)"))
             return codes, scales
 
-        q_staged = load_rows(query, "q_staged", "q_staged")
-        nc.sync.dma_start(out=key_words[:].bitcast(I32), in_=keys_words[0].rearrange("p n t -> p (n t)").bitcast(I32))
-        dq_staged = load_rows(dquery, "dq_staged", "dq_staged")
-
-        key_scale = held.tile([P, SLOTS], U8, name="key_scale", align_bytes=64)
-        nc.vector.tensor_copy(key_scale[:], key_bytes[:].indirect(offsets[:]))
-        q_codes, q_scales = quantise(q_staged, "q")
-        g_staged = load_rows(gout, "g_staged", "q_woven")
-        val_words = held.tile([P, TOKENS], U32, name="val_words", tag="bytes_then_vals")
-        nc.sync.dma_start(out=val_words[:].bitcast(I32), in_=vals_words[0].rearrange("p n t -> p (n t)").bitcast(I32))
-        val_bytes = held.tile([P, TOKENS], U8, name="val_bytes", tag="q_staged", align_bytes=64)
-        nc.vector.memset(val_bytes[:].bitcast(I32), 0)
-        for quad in range(4):
-            nc.scalar.dma_start(out=val_bytes[32 * quad + VAL_ROW : 32 * quad + VAL_ROW + 4, :].bitcast(I32), in_=vals_scales[0, 4 * quad : 4 * quad + 4, :].bitcast(I32))
-        dq_codes, dq_scales = quantise(dq_staged, "dq")
-
-        def gather_words(pool_words, h, name):
-            picked = held.tile([P, HS], U32, name=name + str(h), align_bytes=64)
-            nc.vector.tensor_copy(picked[:], pool_words[:].indirect(offsets[:, h * (HS // 16) : (h + 1) * (HS // 16)]))
+        def gather(pool_tile, dtype, name, tag=None):
+            picked = held.tile([P, SLOTS], dtype, name=name, tag=tag or name, align_bytes=64)
+            nc.vector.tensor_copy(picked[:], pool_tile[:].indirect(offsets[:]))
             return picked
 
         def product(codes, scales, picked, picked_scale, name):
-            acc = psum.tile([P, HS], F32, name=name)
+            acc = psum.tile([P, SLOTS], F32, name=name)
             nc.tensor.matmul_mx(out=acc[:], lhsT=codes[:].bitcast(FP8X4), lhsT_scale=scales[:], rhs=picked[:].bitcast(FP8X4), rhs_scale=picked_scale, start=True, stop=True)
             return acc
 
-        slots = [slice(h * HS, (h + 1) * HS) for h in range(HALVES)]
-        pages = [slice(h * HP, (h + 1) * HP) for h in range(HALVES)]
+        offsets = held.tile([P, SLOTS // 16], U16, name="offsets")
+        key_bytes = held.tile([P, TOKENS], U8, name="key_bytes")
+        key_words = held.tile([P, TOKENS], U32, name="key_words", tag="key_words_slot", align_bytes=64)
+        window = held.tile([P, TOKENS], F32, name="window")
+        q_staged = held.tile([P, PACK, P], F32, name="q_staged")
+        th_col = small("th_col")
+        sharp_col = small("sharp_col")
+        zeros = early.tile([P, 4, 512], F32, name="zeros", offset=0)
+        ones = small("ones", 4)
 
-        keys = [gather_words(key_words, h, "keys") for h in range(HALVES)]
-        a = [product(q_codes, q_scales, keys[h], key_scale[:, slots[h]], "a" + str(h)) for h in range(HALVES)]
-        ta = [product(dq_codes, dq_scales, keys[h], key_scale[:, slots[h]], "ta" + str(h)) for h in range(HALVES)]
+        nc.gpsimd.memset(key_bytes[:].bitcast(I32), 0)
+        nc.gpsimd.memset(zeros[:, :, 0], 0.0)
+        nc.vector.memset(window[:], 0.0)
 
-        base_sum = held.tile([P, TOKENS], F32, name="base_sum", tag="pool_then_base")
-        nc.sync.dma_start(out=base_sum[:], in_=base)
+        load_bytes(nc.scalar, key_bytes, keys_scales, 0)
+        nc.scalar.activation(ones[:], zeros[:, :, 0], ACT.Exp)
+        nc.sync.dma_start(offsets[:], offs)
+        load_rows(q_staged, query)
+        load_words(key_words, keys_words)
+        nc.sync.dma_start(out=th_col[:], in_=th)
+        nc.gpsimd.dma_start(out=sharp_col[:], in_=sharp)
+
+        dq_staged = early.tile([P, PACK, P], F32, name="dq_staged", offset=0)
+        g_staged = early.tile([P, PACK, P], F32, name="g_staged", offset=2048)
+        val_bytes = early.tile([P, TOKENS], U8, name="val_bytes", offset=4096)
+        val_words = early.tile([P, TOKENS], U32, name="val_words", offset=6144)
+        load_rows(dq_staged, dquery)
+        load_words(val_words, vals_words)
+        load_rows(g_staged, gout)
+        nc.vector.memset(val_bytes[:].bitcast(I32), 0)
+        load_bytes(nc.scalar, val_bytes, vals_scales, VAL_ROW)
 
         nth = small("nth")
         sh16 = small("sh16")
         nsh16 = small("nsh16")
+        sh8 = small("sh8")
         nc.gpsimd.tensor_scalar(nth[:], th_col[:], -0.5, 0.0, ALU.mult, ALU.add)
         nc.gpsimd.tensor_scalar(nsh16[:], sharp_col[:], -1.0 / PAGE, 0.0, ALU.mult, ALU.add)
         nc.gpsimd.tensor_scalar(sh16[:], sharp_col[:], 1.0 / PAGE, 0.0, ALU.mult, ALU.add)
+        nc.gpsimd.tensor_scalar(sh8[:], sharp_col[:], 2.0 / PAGE, 0.0, ALU.mult, ALU.add)
 
+        key_scale = gather(key_bytes, U8, "key_scale")
+        keys = gather(key_words, U32, "keys")
+        q_woven = held.tile([P, P, PACK], BF16, name="q_woven", align_bytes=64)
+        dq_woven = held.tile([P, P, PACK], BF16, name="dq_woven", tag="dq_woven", align_bytes=64)
+        q_codes, q_scales = quantise(q_staged, q_woven, "q")
+        dq_codes, dq_scales = quantise(dq_staged, dq_woven, "dq")
+        base_sum = held.tile([P, TOKENS], F32, name="base_sum", tag="dq_woven", align_bytes=64)
+        nc.sync.dma_start(out=base_sum[:], in_=base)
+        val_scale = gather(val_bytes, U8, "val_scale", "key_words_slot")
+        a = product(q_codes, q_scales, keys, key_scale[:], "a")
+        ta = product(dq_codes, dq_scales, keys, key_scale[:], "ta")
 
         t = wide("t")
         tt = wide("tt")
         a_sum = small("a_sum", PAGES)
         ta_sum = small("ta_sum", PAGES)
-        for h in range(HALVES):
-            nc.vector.tensor_reduce(a_sum[:, pages[h]], by_page(a[h][:]), AX.X, ALU.add)
-        for h in range(HALVES):
-            nc.scalar.activation(t[:, slots[h]], a[h][:], ACT.Tanh, bias=nth[:], scale=0.5)
+        nc.vector.tensor_reduce(a_sum[:], by_page(a[:]), AX.X, ALU.add)
+        nc.scalar.activation(t[:], a[:], ACT.Tanh, bias=nth[:], scale=0.5)
         neg_s = small("neg_s", PAGES)
         neg_max = small("neg_max")
         nc.vector.tensor_scalar(neg_s[:], a_sum[:], nsh16[:], None, ALU.mult, ALU.min, accum_out=neg_max[:])
         p = small("p", PAGES)
         z = small("z")
         nc.scalar.activation(p[:], neg_s[:], ACT.Exp, bias=neg_max[:], scale=-1.0, accum_out=z[:])
-        nc.scalar.activation(tt[:], t[:], ACT.Square)
-        for h in range(HALVES):
-            nc.vector.tensor_reduce(ta_sum[:, pages[h]], by_page(ta[h][:]), AX.X, ALU.add)
-        g_codes, g_scales = quantise(g_staged, "g")
+
 
         inv_z = small("inv_z")
-        tp = small("tp", PAGES)
-        tz = small("tz")
+        neg_tp = small("neg_tp", PAGES)
+        neg_tz = small("neg_tz")
         r = small("r", PAGES)
-        ts_mean = small("ts_mean")
+        neg_mean = small("neg_mean")
         v = small("v", PAGES)
         v2s = small("v2s", PAGES)
-        nc.vector.reciprocal(inv_z[:], z[:])
-        nc.vector.scalar_tensor_tensor(tp[:], ta_sum[:], sh16[:], p[:], ALU.mult, ALU.mult, accum_out=tz[:])
         ta_t = wide("ta_t")
-        for h in range(HALVES):
-            nc.vector.tensor_tensor(ta_t[:, slots[h]], ta[h][:], t[:, slots[h]], ALU.mult)
-        nc.vector.tensor_scalar(r[:], p[:], inv_z[:], None, ALU.mult)
-        nc.vector.tensor_scalar(ts_mean[:], tz[:], inv_z[:], None, ALU.mult)
-        nc.vector.tensor_scalar(v[:], ta_sum[:], sh16[:], ts_mean[:], ALU.mult, ALU.subtract)
-        nc.vector.tensor_scalar(v2s[:], v[:], sh16[:], 2.0, ALU.mult, ALU.mult)
         r8 = wide("r8")
+        nc.vector.tensor_reduce(ta_sum[:], by_page(ta[:]), AX.X, ALU.add)
+        nc.vector.reciprocal(inv_z[:], z[:])
+        nc.vector.scalar_tensor_tensor(neg_tp[:], ta_sum[:], nsh16[:], p[:], ALU.mult, ALU.mult, accum_out=neg_tz[:])
+        g_woven = held.tile([P, P, PACK], BF16, name="g_woven", tag="neg_s", align_bytes=64)
+        g_codes, g_scales = quantise(g_staged, g_woven, "g")
+        vals = gather(val_words, U32, "vals", "keys")
+        c = product(g_codes, g_scales, vals, val_scale[VAL_ROW:P, :], "c")
+        nc.vector.tensor_tensor(ta_t[:], ta[:], t[:], ALU.mult)
+        nc.scalar.activation(neg_mean[:], neg_tz[:], ACT.Copy, scale=inv_z[:])
+        nc.scalar.activation(v[:], ta_sum[:], ACT.Identity, bias=neg_mean[:], scale=sh16[:])
+        nc.scalar.activation(tt[:], t[:], ACT.Square)
+        nc.scalar.activation(r[:], p[:], ACT.Copy, scale=inv_z[:])
+        nc.scalar.activation(v2s[:], v[:], ACT.Copy, scale=sh8[:])
         nc.scalar.activation(by_page(r8[:]), spread(r[:]), ACT.Copy, scale=8.0)
 
-        val_scale = held.tile([P, SLOTS], U8, name="val_scale", tag="dq_codes", align_bytes=64)
-        nc.vector.tensor_copy(val_scale[:], val_bytes[:].indirect(offsets[:]))
-        vals = [gather_words(val_words, h, "vals") for h in range(HALVES)]
-        c = [product(g_codes, g_scales, vals[h], val_scale[VAL_ROW:P, slots[h]], "c" + str(h)) for h in range(HALVES)]
-
         shifted = wide("shifted")
-        nc.vector.tensor_tensor(by_page(shifted[:]), by_page(ta_t[:]), spread(v[:]), ALU.subtract)
+        nc.gpsimd.tensor_tensor(by_page(shifted[:]), by_page(ta_t[:]), spread(v[:]), ALU.subtract)
 
         gated = wide("gated")
         curved = wide("curved")
         moved = wide("moved")
+        local = wide("local")
         dr2 = small("dr2", PAGES)
         tdr4 = small("tdr4", PAGES)
-        for h in range(HALVES):
-            nc.vector.scalar_tensor_tensor(curved[:, slots[h]], tt[:, slots[h]], 1.0, c[h][:], ALU.subtract, ALU.mult)
-        for h in range(HALVES):
-            nc.vector.scalar_tensor_tensor(gated[:, slots[h]], t[:, slots[h]], 1.0, c[h][:], ALU.add, ALU.mult)
-        for h in range(HALVES):
-            nc.vector.tensor_tensor(moved[:, slots[h]], ta[h][:], curved[:, slots[h]], ALU.mult)
+        nc.vector.scalar_tensor_tensor(curved[:], tt[:], ones[:, 0:1], c[:], ALU.subtract, ALU.mult)
+        nc.vector.scalar_tensor_tensor(gated[:], t[:], ones[:, 0:1], c[:], ALU.add, ALU.mult)
+        nc.vector.tensor_tensor(moved[:], ta[:], curved[:], ALU.mult)
+        nc.gpsimd.tensor_tensor(local[:], shifted[:], curved[:], ALU.mult)
         nc.vector.tensor_reduce(dr2[:], by_page(gated[:]), AX.X, ALU.add)
-        nc.vector.tensor_reduce(tdr4[:], by_page(moved[:]), AX.X, ALU.add)
 
         r_dr = small("r_dr", PAGES)
         dr_mean = small("dr_mean")
         e = small("e", PAGES)
-        r_e = small("r_e", PAGES)
-        e_mean = small("e_mean")
-        e_centred = small("e_centred", PAGES)
         x = small("x", PAGES)
-        r_tdr = small("r_tdr", PAGES)
-        tdr_mean = small("tdr_mean")
-        local = wide("local")
+        r_x = small("r_x", PAGES)
+        x_mean = small("x_mean")
         nc.vector.scalar_tensor_tensor(r_dr[:], dr2[:], 1.0, r[:], ALU.mult, ALU.mult, accum_out=dr_mean[:])
+        nc.vector.tensor_reduce(tdr4[:], by_page(moved[:]), AX.X, ALU.add)
         nc.vector.scalar_tensor_tensor(e[:], dr2[:], dr_mean[:], v2s[:], ALU.subtract, ALU.mult)
-        nc.vector.scalar_tensor_tensor(r_e[:], e[:], 1.0, r[:], ALU.mult, ALU.mult, accum_out=e_mean[:])
-        nc.vector.tensor_scalar(e_centred[:], e[:], e_mean[:], None, ALU.subtract)
-        nc.vector.scalar_tensor_tensor(r_tdr[:], tdr4[:], nsh16[:], r[:], ALU.mult, ALU.mult, accum_out=tdr_mean[:])
-        nc.vector.scalar_tensor_tensor(x[:], tdr4[:], nsh16[:], e_centred[:], ALU.mult, ALU.add)
-        nc.vector.tensor_tensor(local[:], shifted[:], curved[:], ALU.mult)
+        nc.vector.scalar_tensor_tensor(x[:], tdr4[:], nsh16[:], e[:], ALU.mult, ALU.add)
+        nc.vector.scalar_tensor_tensor(r_x[:], x[:], 1.0, r[:], ALU.mult, ALU.mult, accum_out=x_mean[:])
 
         total = wide("total")
-        nc.vector.scalar_tensor_tensor(by_page(total[:]), spread(x[:]), tdr_mean[:], by_page(local[:]), ALU.subtract, ALU.add)
+        nc.vector.scalar_tensor_tensor(by_page(total[:]), spread(x[:]), x_mean[:], by_page(local[:]), ALU.subtract, ALU.add)
         nc.vector.tensor_tensor(window[:].indirect(offsets[:]), total[:], r8[:], ALU.mult)
 
         start = 0

@@ -20,7 +20,7 @@ SLOTS = 512
 PAGE = 16
 PAGES = SLOTS // PAGE
 VAL_ROW = 4
-OUT_CHUNKS = [256, 512, 512, 512, 256]
+OUT_CHUNKS = [128, 384, 512, 512, 512]
 
 FLOPS = 3 * 2 * 512 * 128 * 512
 
@@ -54,17 +54,14 @@ def tile_attend_hvpagetimessigmoid_s_kernel(tc, query, keys_words, keys_scales, 
         def load_rows(staged, rows):
             nc.sync.dma_start(out=staged[:], in_=rows.rearrange("(p t) q -> p t q", t=PACK))
 
-        def quantise(staged, woven, name):
-            codes = held.tile([P, P], U32, name=name + "_codes", tag=name + "_codes", align_bytes=64)
+        def quantise(staged, woven, codes, name):
             scales = held.tile([P, P], U8, name=name + "_scales", align_bytes=64)
             nc.scalar.copy(out=woven[:], in_=staged[:].rearrange("p t q -> p q t"))
             nc.vector.quantize_mx(out=codes[:].bitcast(FP8X4), scales=scales[:], in_=woven[:].rearrange("p q t -> p (q t)"))
-            return codes, scales
+            return scales
 
-        def gather(pool_tile, dtype, name, tag=None):
-            picked = held.tile([P, SLOTS], dtype, name=name, tag=tag or name, align_bytes=64)
+        def gather(picked, pool_tile):
             nc.vector.tensor_copy(picked[:], pool_tile[:].indirect(offsets[:]))
-            return picked
 
         def product(codes, scales, picked, picked_scale, name):
             acc = psum.tile([P, SLOTS], F32, name=name)
@@ -73,37 +70,37 @@ def tile_attend_hvpagetimessigmoid_s_kernel(tc, query, keys_words, keys_scales, 
 
         offsets = held.tile([P, SLOTS // 16], U16, name="offsets")
         key_bytes = held.tile([P, TOKENS], U8, name="key_bytes")
-        key_words = held.tile([P, TOKENS], U32, name="key_words", tag="key_words_slot", align_bytes=64)
+        key_words = held.tile([P, TOKENS], U32, name="key_words")
         window = held.tile([P, TOKENS], F32, name="window")
         q_staged = held.tile([P, PACK, P], F32, name="q_staged")
+        dq_staged = held.tile([P, PACK, P], F32, name="dq_staged", tag="dq_staged", align_bytes=64)
         th_col = small("th_col")
         sharp_col = small("sharp_col")
-        zeros = early.tile([P, 4, 512], F32, name="zeros", offset=0)
-        ones = small("ones", 4)
+        seeds = early.tile([P, 3, 512], F32, name="seeds", offset=0)
+        ones = small("ones", 3)
 
-        nc.gpsimd.memset(key_bytes[:].bitcast(I32), 0)
-        nc.gpsimd.memset(zeros[:, :, 0], 0.0)
+        nc.vector.memset(key_bytes[:].bitcast(I32), 0)
+        nc.vector.memset(seeds[:, :, 0], 1.0)
         nc.vector.memset(window[:], 0.0)
 
         load_bytes(nc.scalar, key_bytes, keys_scales, 0)
-        nc.scalar.activation(ones[:], zeros[:, :, 0], ACT.Exp)
+        nc.scalar.copy(out=ones[:], in_=seeds[:, :, 0])
         nc.sync.dma_start(offsets[:], offs)
-        load_rows(q_staged, query)
         load_words(key_words, keys_words)
-        nc.sync.dma_start(out=th_col[:], in_=th)
+        load_rows(q_staged, query)
+        load_rows(dq_staged, dquery)
+        nc.gpsimd.dma_start(out=th_col[:], in_=th)
         nc.gpsimd.dma_start(out=sharp_col[:], in_=sharp)
 
-        dq_staged = early.tile([P, PACK, P], F32, name="dq_staged", offset=0)
-        g_staged = early.tile([P, PACK, P], F32, name="g_staged", offset=2048)
-        val_bytes = early.tile([P, TOKENS], U8, name="val_bytes", offset=4096)
-        val_words = early.tile([P, TOKENS], U32, name="val_words", offset=6144)
-        load_rows(dq_staged, dquery)
+        g_staged = early.tile([P, PACK, P], F32, name="g_staged", offset=0)
+        val_bytes = early.tile([P, TOKENS], U8, name="val_bytes", offset=2048)
+        val_words = early.tile([P, TOKENS], U32, name="val_words", offset=4096)
         load_words(val_words, vals_words)
         load_rows(g_staged, gout)
         nc.vector.memset(val_bytes[:].bitcast(I32), 0)
-        load_bytes(nc.scalar, val_bytes, vals_scales, VAL_ROW)
+        load_bytes(nc.sync, val_bytes, vals_scales, VAL_ROW)
 
-        nth = small("nth")
+        nth = early.tile([P, 1], F32, name="nth", offset=12288)
         sh16 = small("sh16")
         nsh16 = small("nsh16")
         sh8 = small("sh8")
@@ -112,27 +109,39 @@ def tile_attend_hvpagetimessigmoid_s_kernel(tc, query, keys_words, keys_scales, 
         nc.gpsimd.tensor_scalar(sh16[:], sharp_col[:], 1.0 / PAGE, 0.0, ALU.mult, ALU.add)
         nc.gpsimd.tensor_scalar(sh8[:], sharp_col[:], 2.0 / PAGE, 0.0, ALU.mult, ALU.add)
 
-        key_scale = gather(key_bytes, U8, "key_scale")
-        keys = gather(key_words, U32, "keys")
+        keys = held.tile([P, SLOTS], U32, name="keys", align_bytes=64)
+        key_scale = held.tile([P, SLOTS], U8, name="key_scale", align_bytes=64)
+        gather(keys, key_words)
+        gather(key_scale, key_bytes)
         q_woven = held.tile([P, P, PACK], BF16, name="q_woven", align_bytes=64)
         dq_woven = held.tile([P, P, PACK], BF16, name="dq_woven", tag="dq_woven", align_bytes=64)
-        q_codes, q_scales = quantise(q_staged, q_woven, "q")
-        dq_codes, dq_scales = quantise(dq_staged, dq_woven, "dq")
+        q_codes = held.tile([P, P], U32, name="q_codes", align_bytes=64)
+        dq_codes = held.tile([P, P], U32, name="dq_codes", align_bytes=64)
+        q_scales = quantise(q_staged, q_woven, q_codes, "q")
+        dq_scales = quantise(dq_staged, dq_woven, dq_codes, "dq")
         base_sum = held.tile([P, TOKENS], F32, name="base_sum", tag="dq_woven", align_bytes=64)
         nc.sync.dma_start(out=base_sum[:], in_=base)
-        val_scale = gather(val_bytes, U8, "val_scale", "key_words_slot")
         a = product(q_codes, q_scales, keys, key_scale[:], "a")
         ta = product(dq_codes, dq_scales, keys, key_scale[:], "ta")
 
+        vals = held.tile([P, SLOTS], U32, name="vals", tag="dq_staged", align_bytes=64)
+        gather(vals, val_words)
+
         t = wide("t")
         tt = wide("tt")
-        a_sum = small("a_sum", PAGES)
-        ta_sum = small("ta_sum", PAGES)
-        nc.vector.tensor_reduce(a_sum[:], by_page(a[:]), AX.X, ALU.add)
         nc.scalar.activation(t[:], a[:], ACT.Tanh, bias=nth[:], scale=0.5)
+        a_sum = early.tile([P, PAGES], F32, name="a_sum", offset=4096)
+        nc.vector.tensor_reduce(a_sum[:], by_page(a[:]), AX.X, ALU.add)
         neg_s = small("neg_s", PAGES)
         neg_max = small("neg_max")
         nc.vector.tensor_scalar(neg_s[:], a_sum[:], nsh16[:], None, ALU.mult, ALU.min, accum_out=neg_max[:])
+        val_scale = early.tile([P, SLOTS], U8, name="val_scale", offset=4096, align_bytes=64)
+        gather(val_scale, val_bytes)
+        g_woven = early.tile([P, P, PACK], BF16, name="g_woven", offset=12288, align_bytes=64)
+        g_codes = early.tile([P, P], U32, name="g_codes", offset=2048, align_bytes=64)
+        g_scales = quantise(g_staged, g_woven, g_codes, "g")
+        c = product(g_codes, g_scales, vals, val_scale[VAL_ROW:P, :], "c")
+        nc.scalar.activation(tt[:], t[:], ACT.Square)
         p = small("p", PAGES)
         z = small("z")
         nc.scalar.activation(p[:], neg_s[:], ACT.Exp, bias=neg_max[:], scale=-1.0, accum_out=z[:])
@@ -145,21 +154,17 @@ def tile_attend_hvpagetimessigmoid_s_kernel(tc, query, keys_words, keys_scales, 
         neg_mean = small("neg_mean")
         v = small("v", PAGES)
         v2s = small("v2s", PAGES)
-        ta_t = wide("ta_t")
-        r8 = wide("r8")
+        ta_t = early.tile([P, SLOTS], F32, name="ta_t", offset=12416)
+        ta_sum = early.tile([P, PAGES], F32, name="ta_sum", offset=12288)
         nc.vector.tensor_reduce(ta_sum[:], by_page(ta[:]), AX.X, ALU.add)
         nc.vector.reciprocal(inv_z[:], z[:])
         nc.vector.scalar_tensor_tensor(neg_tp[:], ta_sum[:], nsh16[:], p[:], ALU.mult, ALU.mult, accum_out=neg_tz[:])
-        g_woven = held.tile([P, P, PACK], BF16, name="g_woven", tag="neg_s", align_bytes=64)
-        g_codes, g_scales = quantise(g_staged, g_woven, "g")
-        vals = gather(val_words, U32, "vals", "keys")
-        c = product(g_codes, g_scales, vals, val_scale[VAL_ROW:P, :], "c")
         nc.vector.tensor_tensor(ta_t[:], ta[:], t[:], ALU.mult)
         nc.scalar.activation(neg_mean[:], neg_tz[:], ACT.Copy, scale=inv_z[:])
         nc.scalar.activation(v[:], ta_sum[:], ACT.Identity, bias=neg_mean[:], scale=sh16[:])
-        nc.scalar.activation(tt[:], t[:], ACT.Square)
         nc.scalar.activation(r[:], p[:], ACT.Copy, scale=inv_z[:])
         nc.scalar.activation(v2s[:], v[:], ACT.Copy, scale=sh8[:])
+        r8 = small("r8", SLOTS, "neg_mean")
         nc.scalar.activation(by_page(r8[:]), spread(r[:]), ACT.Copy, scale=8.0)
 
         shifted = wide("shifted")
@@ -172,7 +177,7 @@ def tile_attend_hvpagetimessigmoid_s_kernel(tc, query, keys_words, keys_scales, 
         dr2 = small("dr2", PAGES)
         tdr4 = small("tdr4", PAGES)
         nc.vector.scalar_tensor_tensor(curved[:], tt[:], ones[:, 0:1], c[:], ALU.subtract, ALU.mult)
-        nc.vector.scalar_tensor_tensor(gated[:], t[:], ones[:, 0:1], c[:], ALU.add, ALU.mult)
+        nc.vector.scalar_tensor_tensor(gated[:], t[:], ones[:, 1:2], c[:], ALU.add, ALU.mult)
         nc.vector.tensor_tensor(moved[:], ta[:], curved[:], ALU.mult)
         nc.gpsimd.tensor_tensor(local[:], shifted[:], curved[:], ALU.mult)
         nc.vector.tensor_reduce(dr2[:], by_page(gated[:]), AX.X, ALU.add)
@@ -183,7 +188,7 @@ def tile_attend_hvpagetimessigmoid_s_kernel(tc, query, keys_words, keys_scales, 
         x = small("x", PAGES)
         r_x = small("r_x", PAGES)
         x_mean = small("x_mean")
-        nc.vector.scalar_tensor_tensor(r_dr[:], dr2[:], 1.0, r[:], ALU.mult, ALU.mult, accum_out=dr_mean[:])
+        nc.vector.scalar_tensor_tensor(r_dr[:], dr2[:], ones[:, 2:3], r[:], ALU.mult, ALU.mult, accum_out=dr_mean[:])
         nc.vector.tensor_reduce(tdr4[:], by_page(moved[:]), AX.X, ALU.add)
         nc.vector.scalar_tensor_tensor(e[:], dr2[:], dr_mean[:], v2s[:], ALU.subtract, ALU.mult)
         nc.vector.scalar_tensor_tensor(x[:], tdr4[:], nsh16[:], e[:], ALU.mult, ALU.add)

@@ -20,7 +20,7 @@ SLOTS = 512
 PAGE = 16
 PAGES = SLOTS // PAGE
 VAL_ROW = 4
-OUT_CHUNKS = [128, 384, 512, 512, 512]
+OUT_CHUNKS = [128, 512, 512, 512, 256, 128]
 
 FLOPS = 3 * 2 * 512 * 128 * 512
 
@@ -151,7 +151,7 @@ def tile_attend_hvpagetimessigmoid_s_kernel(tc, query, keys_words, keys_scales, 
         neg_tp = small("neg_tp", PAGES)
         neg_tz = small("neg_tz")
         r = small("r", PAGES)
-        neg_mean = small("neg_mean")
+        ts = small("ts", PAGES)
         v = small("v", PAGES)
         v2s = small("v2s", PAGES)
         ta_t = early.tile([P, SLOTS], F32, name="ta_t", offset=12416)
@@ -159,12 +159,12 @@ def tile_attend_hvpagetimessigmoid_s_kernel(tc, query, keys_words, keys_scales, 
         nc.vector.tensor_reduce(ta_sum[:], by_page(ta[:]), AX.X, ALU.add)
         nc.vector.reciprocal(inv_z[:], z[:])
         nc.vector.scalar_tensor_tensor(neg_tp[:], ta_sum[:], nsh16[:], p[:], ALU.mult, ALU.mult, accum_out=neg_tz[:])
+        nc.scalar.activation(ts[:], ta_sum[:], ACT.Copy, scale=sh16[:])
+        nc.vector.scalar_tensor_tensor(v[:], neg_tz[:].to_broadcast([P, PAGES]), inv_z[:], ts[:], ALU.mult, ALU.add)
         nc.vector.tensor_tensor(ta_t[:], ta[:], t[:], ALU.mult)
-        nc.scalar.activation(neg_mean[:], neg_tz[:], ACT.Copy, scale=inv_z[:])
-        nc.scalar.activation(v[:], ta_sum[:], ACT.Identity, bias=neg_mean[:], scale=sh16[:])
         nc.scalar.activation(r[:], p[:], ACT.Copy, scale=inv_z[:])
         nc.scalar.activation(v2s[:], v[:], ACT.Copy, scale=sh8[:])
-        r8 = small("r8", SLOTS, "neg_mean")
+        r8 = wide("r8")
         nc.scalar.activation(by_page(r8[:]), spread(r[:]), ACT.Copy, scale=8.0)
 
         shifted = wide("shifted")

from contextlib import ExitStack

import concourse.mybir as mybir

F32 = mybir.dt.float32
BF16 = mybir.dt.bfloat16
I32 = mybir.dt.int32
U32 = mybir.dt.uint32
U16 = mybir.dt.uint16
U8 = mybir.dt.uint8
FP8X4 = mybir.dt.float8_e4m3fn_x4
ALU = mybir.AluOpType
ACT = mybir.ActivationFunctionType
AX = mybir.AxisListType

P = 128
PACK = 4
TOKENS = 2048
SLOTS = 512
PAGE = 16
PAGES = SLOTS // PAGE
VAL_ROW = 4
OUT_CHUNKS = [128, 512, 512, 512, 256, 128]

FLOPS = 3 * 2 * 512 * 128 * 512


def tile_attend_hvpagetimessigmoid_s_kernel(tc, query, keys_words, keys_scales, th, sharp, gout, vals_words, vals_scales, dquery, base, offs, out):
    nc = tc.nc
    with ExitStack() as ctx:
        held = ctx.enter_context(tc.tile_pool(name="held", bufs=1))
        early = ctx.enter_context(tc.tile_pool(name="early", bufs=1))
        psum = ctx.enter_context(tc.psum_pool(name="psum", bufs=1))

        def small(name, width=1, tag=None):
            return held.tile([P, width], F32, name=name, tag=tag or name, align_bytes=64)

        def wide(name):
            return held.tile([P, SLOTS], F32, name=name)

        def by_page(ap):
            return ap.rearrange("p (g j) -> p g j", j=PAGE)

        def spread(ap):
            return ap.unsqueeze(2).to_broadcast([P, PAGES, PAGE])

        def load_words(pool_words, words):
            nc.sync.dma_start(out=pool_words[:].bitcast(I32), in_=words[0].rearrange("p n t -> p (n t)").bitcast(I32))

        def load_bytes(queue, pool_bytes, scale_rows, first):
            for quad in range(4):
                queue.dma_start(out=pool_bytes[32 * quad + first : 32 * quad + first + 4, :].bitcast(I32), in_=scale_rows[0, 4 * quad : 4 * quad + 4, :].bitcast(I32))

        def load_rows(staged, rows):
            nc.sync.dma_start(out=staged[:], in_=rows.rearrange("(p t) q -> p t q", t=PACK))

        def quantise(staged, woven, codes, name):
            scales = held.tile([P, P], U8, name=name + "_scales", align_bytes=64)
            nc.scalar.copy(out=woven[:], in_=staged[:].rearrange("p t q -> p q t"))
            nc.vector.quantize_mx(out=codes[:].bitcast(FP8X4), scales=scales[:], in_=woven[:].rearrange("p q t -> p (q t)"))
            return scales

        def gather(picked, pool_tile):
            nc.vector.tensor_copy(picked[:], pool_tile[:].indirect(offsets[:]))

        def product(codes, scales, picked, picked_scale, name):
            acc = psum.tile([P, SLOTS], F32, name=name)
            nc.tensor.matmul_mx(out=acc[:], lhsT=codes[:].bitcast(FP8X4), lhsT_scale=scales[:], rhs=picked[:].bitcast(FP8X4), rhs_scale=picked_scale, start=True, stop=True)
            return acc

        offsets = held.tile([P, SLOTS // 16], U16, name="offsets")
        key_bytes = held.tile([P, TOKENS], U8, name="key_bytes")
        key_words = held.tile([P, TOKENS], U32, name="key_words")
        window = held.tile([P, TOKENS], F32, name="window")
        q_staged = held.tile([P, PACK, P], F32, name="q_staged")
        dq_staged = held.tile([P, PACK, P], F32, name="dq_staged", tag="dq_staged", align_bytes=64)
        th_col = small("th_col")
        sharp_col = small("sharp_col")
        seeds = early.tile([P, 3, 512], F32, name="seeds", offset=0)
        ones = small("ones", 3)

        nc.vector.memset(key_bytes[:].bitcast(I32), 0)
        nc.vector.memset(seeds[:, :, 0], 1.0)
        nc.vector.memset(window[:], 0.0)

        load_bytes(nc.scalar, key_bytes, keys_scales, 0)
        nc.scalar.copy(out=ones[:], in_=seeds[:, :, 0])
        nc.sync.dma_start(offsets[:], offs)
        load_words(key_words, keys_words)
        load_rows(q_staged, query)
        load_rows(dq_staged, dquery)
        nc.gpsimd.dma_start(out=th_col[:], in_=th)
        nc.gpsimd.dma_start(out=sharp_col[:], in_=sharp)

        g_staged = early.tile([P, PACK, P], F32, name="g_staged", offset=0)
        val_bytes = early.tile([P, TOKENS], U8, name="val_bytes", offset=2048)
        val_words = early.tile([P, TOKENS], U32, name="val_words", offset=4096)
        load_words(val_words, vals_words)
        load_rows(g_staged, gout)
        nc.vector.memset(val_bytes[:].bitcast(I32), 0)
        load_bytes(nc.sync, val_bytes, vals_scales, VAL_ROW)

        nth = early.tile([P, 1], F32, name="nth", offset=12288)
        sh16 = small("sh16")
        nsh16 = small("nsh16")
        sh8 = small("sh8")
        nc.gpsimd.tensor_scalar(nth[:], th_col[:], -0.5, 0.0, ALU.mult, ALU.add)
        nc.gpsimd.tensor_scalar(nsh16[:], sharp_col[:], -1.0 / PAGE, 0.0, ALU.mult, ALU.add)
        nc.gpsimd.tensor_scalar(sh16[:], sharp_col[:], 1.0 / PAGE, 0.0, ALU.mult, ALU.add)
        nc.gpsimd.tensor_scalar(sh8[:], sharp_col[:], 2.0 / PAGE, 0.0, ALU.mult, ALU.add)

        keys = held.tile([P, SLOTS], U32, name="keys", align_bytes=64)
        key_scale = held.tile([P, SLOTS], U8, name="key_scale", align_bytes=64)
        gather(keys, key_words)
        gather(key_scale, key_bytes)
        q_woven = held.tile([P, P, PACK], BF16, name="q_woven", align_bytes=64)
        dq_woven = held.tile([P, P, PACK], BF16, name="dq_woven", tag="dq_woven", align_bytes=64)
        q_codes = held.tile([P, P], U32, name="q_codes", align_bytes=64)
        dq_codes = held.tile([P, P], U32, name="dq_codes", align_bytes=64)
        q_scales = quantise(q_staged, q_woven, q_codes, "q")
        dq_scales = quantise(dq_staged, dq_woven, dq_codes, "dq")
        base_sum = held.tile([P, TOKENS], F32, name="base_sum", tag="dq_woven", align_bytes=64)
        nc.sync.dma_start(out=base_sum[:], in_=base)
        a = product(q_codes, q_scales, keys, key_scale[:], "a")
        ta = product(dq_codes, dq_scales, keys, key_scale[:], "ta")

        vals = held.tile([P, SLOTS], U32, name="vals", tag="dq_staged", align_bytes=64)
        gather(vals, val_words)

        t = wide("t")
        tt = wide("tt")
        nc.scalar.activation(t[:], a[:], ACT.Tanh, bias=nth[:], scale=0.5)
        a_sum = early.tile([P, PAGES], F32, name="a_sum", offset=4096)
        nc.vector.tensor_reduce(a_sum[:], by_page(a[:]), AX.X, ALU.add)
        neg_s = small("neg_s", PAGES)
        neg_max = small("neg_max")
        nc.vector.tensor_scalar(neg_s[:], a_sum[:], nsh16[:], None, ALU.mult, ALU.min, accum_out=neg_max[:])
        val_scale = early.tile([P, SLOTS], U8, name="val_scale", offset=4096, align_bytes=64)
        gather(val_scale, val_bytes)
        g_woven = early.tile([P, P, PACK], BF16, name="g_woven", offset=12288, align_bytes=64)
        g_codes = early.tile([P, P], U32, name="g_codes", offset=2048, align_bytes=64)
        g_scales = quantise(g_staged, g_woven, g_codes, "g")
        c = product(g_codes, g_scales, vals, val_scale[VAL_ROW:P, :], "c")
        nc.scalar.activation(tt[:], t[:], ACT.Square)
        p = small("p", PAGES)
        z = small("z")
        nc.scalar.activation(p[:], neg_s[:], ACT.Exp, bias=neg_max[:], scale=-1.0, accum_out=z[:])


        inv_z = small("inv_z")
        neg_tp = small("neg_tp", PAGES)
        neg_tz = small("neg_tz")
        r = small("r", PAGES)
        ts = small("ts", PAGES)
        v = small("v", PAGES)
        v2s = small("v2s", PAGES)
        ta_t = early.tile([P, SLOTS], F32, name="ta_t", offset=12416)
        ta_sum = early.tile([P, PAGES], F32, name="ta_sum", offset=12288)
        nc.vector.tensor_reduce(ta_sum[:], by_page(ta[:]), AX.X, ALU.add)
        nc.vector.reciprocal(inv_z[:], z[:])
        nc.vector.scalar_tensor_tensor(neg_tp[:], ta_sum[:], nsh16[:], p[:], ALU.mult, ALU.mult, accum_out=neg_tz[:])
        nc.scalar.activation(ts[:], ta_sum[:], ACT.Copy, scale=sh16[:])
        nc.vector.scalar_tensor_tensor(v[:], neg_tz[:].to_broadcast([P, PAGES]), inv_z[:], ts[:], ALU.mult, ALU.add)
        nc.vector.tensor_tensor(ta_t[:], ta[:], t[:], ALU.mult)
        nc.scalar.activation(r[:], p[:], ACT.Copy, scale=inv_z[:])
        nc.scalar.activation(v2s[:], v[:], ACT.Copy, scale=sh8[:])
        r8 = wide("r8")
        nc.scalar.activation(by_page(r8[:]), spread(r[:]), ACT.Copy, scale=8.0)

        shifted = wide("shifted")
        nc.gpsimd.tensor_tensor(by_page(shifted[:]), by_page(ta_t[:]), spread(v[:]), ALU.subtract)

        gated = wide("gated")
        curved = wide("curved")
        moved = wide("moved")
        local = wide("local")
        dr2 = small("dr2", PAGES)
        tdr4 = small("tdr4", PAGES)
        nc.vector.scalar_tensor_tensor(curved[:], tt[:], ones[:, 0:1], c[:], ALU.subtract, ALU.mult)
        nc.vector.scalar_tensor_tensor(gated[:], t[:], ones[:, 1:2], c[:], ALU.add, ALU.mult)
        nc.vector.tensor_tensor(moved[:], ta[:], curved[:], ALU.mult)
        nc.gpsimd.tensor_tensor(local[:], shifted[:], curved[:], ALU.mult)
        nc.vector.tensor_reduce(dr2[:], by_page(gated[:]), AX.X, ALU.add)

        r_dr = small("r_dr", PAGES)
        dr_mean = small("dr_mean")
        e = small("e", PAGES)
        x = small("x", PAGES)
        r_x = small("r_x", PAGES)
        x_mean = small("x_mean")
        nc.vector.scalar_tensor_tensor(r_dr[:], dr2[:], ones[:, 2:3], r[:], ALU.mult, ALU.mult, accum_out=dr_mean[:])
        nc.vector.tensor_reduce(tdr4[:], by_page(moved[:]), AX.X, ALU.add)
        nc.vector.scalar_tensor_tensor(e[:], dr2[:], dr_mean[:], v2s[:], ALU.subtract, ALU.mult)
        nc.vector.scalar_tensor_tensor(x[:], tdr4[:], nsh16[:], e[:], ALU.mult, ALU.add)
        nc.vector.scalar_tensor_tensor(r_x[:], x[:], 1.0, r[:], ALU.mult, ALU.mult, accum_out=x_mean[:])

        total = wide("total")
        nc.vector.scalar_tensor_tensor(by_page(total[:]), spread(x[:]), x_mean[:], by_page(local[:]), ALU.subtract, ALU.add)
        nc.vector.tensor_tensor(window[:].indirect(offsets[:]), total[:], r8[:], ALU.mult)

        start = 0
        for n, width in enumerate(OUT_CHUNKS):
            cols = slice(start, start + width)
            nc.vector.tensor_tensor(base_sum[:, cols], base_sum[:, cols], window[:, cols], ALU.add)
            queue = nc.sync if n % 2 == 0 else nc.scalar
            queue.dma_start(out=out[:, cols], in_=base_sum[:, cols])
            start = start + width
